import numpy as np, ml_dtypes
CORES = [129,145,193,257,273,321,385,401,449]
N = 9
import mx_ref
NC, G, D = 128, 2, 2
C = np.float32(0.019)
BF = ml_dtypes.bfloat16
def cut(t, i, w=512):
    return t[:, w * i:w * i + w]
def tile(rs):
    return np.stack(rs, axis=2).reshape(128, -1).astype(BF)
def act(Z):
    return [np.maximum(s * z, 0) * C for z in Z for s in (1, -1)]
def taps(w, i, e):
    return mx_ref.matmul(mx_ref.quantize(cut(w, 2 * i)), mx_ref.quantize(e[:, :4 * NC])) + mx_ref.matmul(mx_ref.quantize(cut(w, 2 * i + 1)), mx_ref.quantize(e[:, 4 * D:4 * D + 4 * NC]))
def setup_inputs(rng):
    def f(*shape):
        return mx_ref.flush((rng.standard_normal(shape, dtype=np.float32) * np.exp2(rng.integers(-2, 3, shape[:-1] + (1,)))).astype(BF))
    return {"x": f(N, 128, 4 * NC), "wa": np.broadcast_to(f(1, 128, 2 * G * 512), (N, 128, 2 * G * 512)).copy(), "wb": f(N, 128, 2 * 512)}
def setup_inputs_blocks(rng):
    d = setup_inputs(rng)
    for k in ("x", "wb"): d[k] = mx_ref.spread(d[k], rng, 2)
    return d
def setup_inputs_wide(rng):
    d = setup_inputs(rng)
    for k in ("wb",): d[k] = mx_ref.flush((d[k].astype(np.float32) * np.exp2(rng.integers(-6, 7, (N, 1, 1))).astype(np.float32)).astype(BF))
    return d
def setup_inputs_zeros(rng):
    d = setup_inputs(rng); v = d["x"].reshape(N, 128, -1, 4).copy()
    v[np.broadcast_to((rng.random((N, 1, v.shape[2], 1)) < 0.33), v.shape)] = 0
    d["x"] = v.reshape(d["x"].shape)
    return d
def reference(x, wa, wb):
    edge = lambda t, r: np.concatenate([t[(r - 1) % N][:, 4 * (NC - D):], t[r]], axis=1)
    u = [tile(act([taps(wa[r], i, edge(x, r)) for i in range(G)])) for r in range(N)]
    y = np.zeros((N, 128, NC), np.float32)
    for r in range(N):
        y[r] = taps(wb[r], 0, edge(u, r))
    return {"y": y}

import numpy as np
from concourse.bass import DstId, RemoteDMATransfer
from concourse.mybir import dt, AluOpType

NC, D = 128, 2
H = 2 * D
OWN = 16
C = float(np.float32(0.019))
SIM_CORES = 512
W8 = "float8_e4m3fn_x4"

SCRATCH = {
    "xt": ("sbuf", [128, 4 * (NC + D)], "bfloat16"),
    "xq": ("sbuf", [128, OWN + NC + D], W8), "xs": ("sbuf", [128, OWN + NC + D], "uint8"),
    "at": ("sbuf", [128, 16 * NC], "bfloat16"), "aq": ("sbuf", [128, 4 * NC], W8), "asc": ("sbuf", [128, 4 * NC], "uint8"),
    "bt": ("sbuf", [128, 8 * NC], "bfloat16"), "bq": ("sbuf", [128, 2 * NC], W8), "bsc": ("sbuf", [128, 2 * NC], "uint8"),
    "ut": ("sbuf", [128, 4 * (H + NC + D)], "bfloat16"),
    "eq": ("sbuf", [128, NC + D], W8), "es": ("sbuf", [128, NC + D], "uint8"),
    "uq": ("sbuf", [128, NC + D], W8), "us": ("sbuf", [128, NC + D], "uint8"),
    "ye": ("sbuf", [128, NC], "float32"), "yl": ("sbuf", [128, NC], "float32"),
    "rq": ("sbuf", [128, H], W8), "rs": ("sbuf", [128, 4 * H], "uint8"),
    "ze0": ("psum", [128, 512], "float32"), "ze1": ("psum", [128, 512], "float32"), "pe": ("psum", [128, 512], "float32"),
    "zl0": ("psum", [128, 512], "float32"), "zl1": ("psum", [128, 512], "float32"), "pl": ("psum", [128, 512], "float32"),
}
SEMAPHORES = ["fill", "l_x", "l_a0", "l_a1", "l_b", "q_x", "q_a0", "q_a1", "q_b",
              "ez0", "ez1", "e_act", "e_q", "e_p", "e_y", "e_st",
              "lz0", "lz1", "l_act", "l_q", "l_p", "l_y", "l_st", "arr", "sent"]


def engines(topo, src, dst):
    m = topo.mask(src, dst)
    return [1 << i for i in range(16) if m >> i & 1]


def relays(T, topo, src, dst):
    return [c for c in range(SIM_CORES)
            if topo.chip(c) == topo.chip(src) and topo.die(c) == topo.die(src) == topo.die(dst)
            and topo.rack(topo.host(c)) == topo.rack(topo.host(dst)) != topo.rack(topo.host(src))
            and T.rank_of(c) is None and topo.same_plane(c, dst)
            and topo.may_write(src, c) and topo.may_write(c, dst)][:2]


def put(g, T, topo, core, dst, out, in_, mask):
    rid, pid = topo.addr(dst, core)
    g.remote_dma(out, in_, T.sem.arr, T.sem.sent, pid, rid, mask)


def relay_program(g, core, T, topo):
    for r, dst in enumerate(T.cores):
        src = T.cores[r - 1]
        if topo.may_write(src, dst):
            continue
        two = relays(T, topo, src, dst)
        if core not in two:
            continue
        es = engines(topo, core, dst)[0::2]
        g.wait_ge(T.sem.arr, len(engines(topo, src, core)) // 2)
        if core == two[0]:
            put(g, T, topo, core, dst, T.xq[:, OWN - H:OWN].bitcast(dt.uint8), T.rq[:, 0:H].bitcast(dt.uint8), sum(es))
        else:
            put(g, T, topo, core, dst, T.xs[:, OWN - H:OWN], T.rs[:, 3 * H:4 * H], sum(es))
        g.wait_ge(T.sem.sent, len(es))


def send_halo(g, core, dst, T, topo):
    g.wait_ge(T.sem.q_x, 1)
    end = OWN + NC
    codes = T.xq[:, end - H:end].bitcast(dt.uint8)
    if topo.may_write(core, dst):
        es = engines(topo, core, dst)
        put(g, T, topo, core, dst, T.xq[:, OWN - H:OWN].bitcast(dt.uint8), codes, sum(es[0::2]))
        put(g, T, topo, core, dst, T.xs[:, OWN - H:OWN], T.xs[:, end - H:end], sum(es[1::2]))
        return len(es)
    two = relays(T, topo, core, dst)
    n, ts = 0, []
    for k, (c, d, s) in enumerate(((two[0], T.rq[:, 0:H].bitcast(dt.uint8), codes),
                                   (two[1], T.rs[:, 0:4 * H], T.xs[:, end - 4 * H:end]))):
        es = engines(topo, core, c)[k::2]
        rid, pid = topo.addr(c, core)
        ts.append(RemoteDMATransfer(dst_ids=[DstId(rid=rid, pnc=pid)], dma_engine_mask=sum(es), remote_sem=T.sem.arr, src=s, dst=d))
        n += len(es)
    g.remote_dma_fused(ts, local_sem=T.sem.sent)
    return n


def rank_program(g, core, T, topo):
    rank = T.rank_of(core)
    if rank is None:
        return relay_program(g, core, T, topo)
    S, V, PE, n = T.sem, g.vector, g.tensor, len(T.cores)
    nxt, prv = T.cores[(rank + 1) % n], T.cores[rank - 1]
    before = not topo.may_write(core, nxt)
    late = not topo.may_write(prv, core)

    def load(q, out, in_, sem):
        q.dma_start(out, in_).then_inc(sem, 16)
    nx = NC + D if late else NC
    load(g.sync, T.xt[:, 0:4 * NC], T.x[:, :], S.l_x)
    if late:
        load(g.scalar, T.xt[:, 4 * NC:4 * nx], T.x[:, 0:4 * D], S.l_x)
    q2 = g.sync if before else g.scalar
    load(q2, T.at[:, 0:8 * NC], T.wa[:, 0:8 * NC], S.l_a0)
    load(g.sync, T.at[:, 8 * NC:16 * NC], T.wa[:, 8 * NC:16 * NC], S.l_a1)

    sent = send_halo(g, core, nxt, T, topo)
    if before:
        g.sync.wait_ge(S.sent, sent)
    else:
        g.wait_ge(S.sent, sent)
    load(g.sync, T.bt[:, :], T.wb[:, :], S.l_b)

    if late:
        V.memset(T.ut[:, 4 * (NC + D):4 * (H + NC + D)], 0.0).then_inc(S.fill, 1)
    V.wait_ge(S.l_x, 32 if late else 16)
    V.quantize_mx(T.xq[:, OWN:OWN + nx], T.xs[:, OWN:OWN + nx], T.xt[:, 0:4 * nx]).then_inc(S.q_x, 1)
    for i, (ld, qd) in enumerate(((S.l_a0, S.q_a0), (S.l_a1, S.q_a1))):
        a, b = 2 * NC * i, 2 * NC * (i + 1)
        V.wait_ge(ld, 16)
        V.quantize_mx(T.aq[:, a:b], T.asc[:, a:b], T.at[:, 4 * a:4 * b]).then_inc(qd, 1)

    def quantise_wb():
        V.wait_ge(S.l_b, 16)
        V.quantize_mx(T.bq[:, :], T.bsc[:, :], T.bt[:, :]).then_inc(S.q_b, 1)

    def layer1(i, out, first, w, done):
        for t in range(2):
            k, a = NC * (2 * i + t), first + D * t
            m = PE.matmul_mx(out[:, 0:w], T.aq[:, k:k + NC], T.asc[:, k:k + NC], T.xq[:, a:a + w], T.xs[:, a:a + w], t == 0, t == 1)
        m.then_inc(done, 1)

    def relu_pair(i, z, k0, k1, ready, done):
        V.wait_ge(ready, 1)
        for s in range(2):
            b = 2 * i + s
            V.tensor_scalar(out=T.ut[:, 4 * k0 + b:4 * k1:4], in0=z[:, 0:k1 - k0], scalar1=(-C if s else C), scalar2=0.0,
                            op0=AluOpType.mult, op1=AluOpType.max).then_inc(done, 1)

    def layer2(out, q, s, done):
        for t in range(2):
            m = PE.matmul_mx(out[:, 0:NC], T.bq[:, NC * t:NC * t + NC], T.bsc[:, NC * t:NC * t + NC],
                             q[:, D * t:D * t + NC], s[:, D * t:D * t + NC], t == 0, t == 1)
        m.then_inc(done, 1)

    PE.wait_ge(S.q_x, 1)
    PE.wait_ge(S.q_a0, 1)
    if late:
        layer1(0, T.ze0, OWN, NC, S.ez0)
        PE.wait_ge(S.q_a1, 1)
        layer1(1, T.ze1, OWN, NC, S.ez1)
        relu_pair(0, T.ze0, H, NC + D, S.ez0, S.e_act)
        relu_pair(1, T.ze1, H, NC + D, S.ez1, S.e_act)
        V.wait_ge(S.fill, 1)
        V.wait_ge(S.e_act, 4)
        V.quantize_mx(T.eq[:, :], T.es[:, :], T.ut[:, 4 * H:4 * (H + NC + D)]).then_inc(S.e_q, 1)
        quantise_wb()
        PE.wait_ge(S.e_q, 1)
        PE.wait_ge(S.q_b, 1)
        layer2(T.pe, T.eq, T.es, S.e_p)
        V.wait_ge(S.e_p, 1)
        V.tensor_copy(T.ye[:, 0:NC - H], T.pe[:, 0:NC - H]).then_inc(S.e_y, 1)
        g.scalar.wait_ge(S.e_y, 1)
        g.scalar.dma_start(T.y[:, H:NC], T.ye[:, 0:NC - H]).then_inc(S.e_st, 16)
    elif not before:
        quantise_wb()

    if late:
        arrive = sum(len(engines(topo, c, core)[0::2]) for c in relays(T, topo, prv, core))
    else:
        arrive = len(engines(topo, prv, core))
    w1 = NC if late else NC + D
    u1 = H if late else NC + D
    y1 = H if late else NC
    PE.wait_ge(S.arr, arrive)
    layer1(0, T.zl0, OWN - H, w1, S.lz0)
    if not late:
        PE.wait_ge(S.q_a1, 1)
    layer1(1, T.zl1, OWN - H, w1, S.lz1)
    relu_pair(0, T.zl0, 0, u1, S.lz0, S.l_act)
    relu_pair(1, T.zl1, 0, u1, S.lz1, S.l_act)
    V.wait_ge(S.l_act, 4)
    V.quantize_mx(T.uq[:, :], T.us[:, :], T.ut[:, 0:4 * (NC + D)]).then_inc(S.l_q, 1)
    if before:
        quantise_wb()
    PE.wait_ge(S.l_q, 1)
    if not late:
        PE.wait_ge(S.q_b, 1)
    layer2(T.pl, T.uq, T.us, S.l_p)
    V.wait_ge(S.l_p, 1)
    V.tensor_copy(T.yl[:, 0:y1], T.pl[:, 0:y1]).then_inc(S.l_y, 1)
    g.sync.wait_ge(S.l_y, 1)
    g.sync.dma_start(T.y[:, 0:y1], T.yl[:, 0:y1]).then_inc(S.l_st, 16)
    g.sync.wait_ge(S.l_st, 16)
    if late:
        g.scalar.wait_ge(S.e_st, 16)
